import numpy as np
import ml_dtypes


def mxq(x, axis, fmt="e4m3"):
    dtype, down = {"e4m3": (ml_dtypes.float8_e4m3fn, 7), "e5m2": (ml_dtypes.float8_e5m2, 14)}[fmt]
    v = np.moveaxis(np.asarray(x, np.float32).astype(ml_dtypes.bfloat16).astype(np.float64), axis, -1)
    blocks = v.reshape(v.shape[:-1] + (-1, 32))
    amax = np.abs(blocks).max(-1, keepdims=True)
    byte = np.maximum(np.where(amax > 0, np.frexp(amax)[1] - 1 + 127, 0) - down, 1)
    scale = np.exp2(byte - 127.0)
    codes = (blocks / scale).astype(np.float32).astype(dtype).astype(np.float64)
    return np.moveaxis((codes * scale).reshape(v.shape), -1, axis)


WIDE = False


def mx_kscale(k):
    if not WIDE:
        return np.ones(k)
    levels = np.array([30, -30])
    if k % 512:
        return np.exp2(np.random.permutation(np.resize(levels, k // 32))).repeat(32)
    a = np.empty((k // 512, 16))
    for p in range(k // 512):
        a[p, :8] = np.random.permutation(np.resize(levels, 8))
        for g in range(8):
            far = levels[np.abs(levels - a[p, g]) >= 10]
            a[p, g + 8] = far[np.random.randint(len(far))]
    return np.exp2(a.ravel()).repeat(32)


def f64(x):
    return np.asarray(x).astype(np.float64)


def striped(idx):
    return np.tile(np.asarray(idx).reshape(-1, 16).T, (8, 1)).astype(np.uint16)


def unstriped(offs):
    return offs[:16].T.reshape(-1).astype(np.int64)


K, J, N, T, V = 256, 1024, 256, 2048, 2048


def setup_inputs():
    n = np.random.standard_normal
    idx = np.random.permutation(T)[:J]
    idx2 = np.random.permutation(V)[:J]
    fj = mx_kscale(J)
    return {
        "xf": (n((K, T))).astype(np.float32),
        "ra": (np.random.uniform(0.5, 1.5, (1, J)) * fj).astype(np.float32),
        "ow": (n((K, J)) * 0.7).astype(np.float32),
        "gt": (n((N, V)) * np.exp(0.5 * n((1, V)))).astype(np.float32),
        "rb": (np.random.uniform(0.5, 1.5, (1, J)) / fj).astype(np.float32),
        "pr": (n((N, J))).astype(np.float32),
        "old": (1.0 * n((K, N))).astype(np.float32),
        "offs": striped(idx),
        "offs2": striped(idx2),
    }


def reference(xf, ra, ow, gt, rb, pr, old, offs, offs2):
    idx = unstriped(offs)
    idx2 = unstriped(offs2)
    us = (f64(xf)[:, idx] - f64(ow)) * f64(ra)
    uj = us.T
    gs = (f64(gt)[:, idx2] - f64(pr)) * f64(rb)
    gj = gs.T
    ujq = mxq(uj, 0, "e4m3")
    gjq = mxq(gj, 0, "e5m2")
    w = ujq.T @ gjq
    pk1 = np.max(np.abs(w), axis=1, keepdims=True)
    y = w / (pk1 + 2.0) - 0.3 * f64(old)
    return y

@@ -1,0 +1,195 @@
+from contextlib import ExitStack
+
+import concourse.mybir as mybir
+from concourse.masks import make_identity
+
+K, J, N, T = 256, 1024, 256, 2048
+FLOPS = 2 * K * N * J
+
+F32 = mybir.dt.float32
+BF16 = mybir.dt.bfloat16
+U32 = mybir.dt.uint32
+U16 = mybir.dt.uint16
+U8 = mybir.dt.uint8
+E4M3X4 = mybir.dt.float8_e4m3fn_x4
+E5M2X4 = mybir.dt.float8_e5m2_x4
+ALU = mybir.AluOpType
+ACT = mybir.ActivationFunctionType
+
+P = 128
+PACK = 4
+RUN = 8
+SPAN = P * PACK
+PASSES = J // SPAN
+
+
+def tile_list_moment_offset_errors_rowpeaks_kernel(tc, xf, ra, ow, gt, rb, pr, old, offs, offs2, out):
+    nc = tc.nc
+    with ExitStack() as ctx:
+        lists = ctx.enter_context(tc.tile_pool(name="lists", bufs=1))
+        keep = ctx.enter_context(tc.tile_pool(name="keep", bufs=1))
+        psum = ctx.enter_context(tc.psum_pool(name="psum", bufs=1))
+
+        x_list = lists.tile([P, J // 16], U16, name="x_list")
+        g_list = lists.tile([P, J // 16], U16, name="g_list")
+
+        def rows(r):
+            return slice(r * P, (r + 1) * P)
+
+        def load_table(name, src, r):
+            table = keep.tile([P, T], F32, name="%s_table%d" % (name, r))
+            nc.sync.dma_start(out=table[:], in_=src[rows(r), :])
+            return table
+
+        def load_own(name, src, r, pieces):
+            width = J // pieces
+            tiles = []
+            for c in range(pieces):
+                own = keep.tile([P, width], F32, name="%s_own%d_%d" % (name, r, c))
+                nc.sync.dma_start(out=own[:], in_=src[rows(r), c * width : (c + 1) * width])
+                tiles.append(own)
+            return [tiles[a * SPAN // width][:, a * SPAN % width : a * SPAN % width + SPAN] for a in range(PASSES)]
+
+        weight_rows = keep.tile([P, P], F32, name="weight_rows")
+        nc.vector.memset(weight_rows[:], 0.0)
+        ident = keep.tile([P, P], F32, name="ident")
+        make_identity(nc, ident[:])
+
+        g_table0 = load_table("g", gt, 0)
+        nc.sync.dma_start(g_list[:], offs2)
+        weight_raw = keep.tile([P, P], F32, name="weight_raw")
+        first_weights = []
+        for side, vec in enumerate((ra, rb)):
+            first = keep.tile([P, PACK], F32, name="first_weights%d" % side)
+            nc.sync.dma_start(out=first[:], in_=vec[:, 0:SPAN].rearrange("o (p t) -> (o p) t", t=PACK))
+            first_weights.append(first)
+            nc.sync.dma_start(
+                out=weight_raw[side * PACK : (side + 1) * PACK, :].rearrange("t (g i) -> t g i", i=RUN),
+                in_=vec[:, SPAN:J].rearrange("o (g t i) -> t (o g) i", t=PACK, i=RUN),
+            )
+        nc.vector.tensor_copy(out=weight_rows[0 : 2 * PACK, :], in_=weight_raw[0 : 2 * PACK, :])
+        g_own0 = load_own("g", pr, 0, 1)
+        g_table1 = load_table("g", gt, 1)
+        g_own1 = load_own("g", pr, 1, 1)
+        nc.sync.dma_start(x_list[:], offs)
+        x_table0 = load_table("x", xf, 0)
+        x_own0 = load_own("x", ow, 0, 1)
+        x_table1 = load_table("x", xf, 1)
+        x_own1 = load_own("x", ow, 1, PASSES)
+        old_raw = keep.tile([P, K // P, N], F32, name="old_raw")
+        nc.sync.dma_start(out=old_raw[:], in_=old.rearrange("(r p) n -> p r n", p=P))
+
+        weight_bank = psum.tile([P, P], F32, name="weight_bank")
+        nc.tensor.transpose(weight_bank[:], weight_rows[:], ident[:])
+        second_weights = keep.tile([P, 2 * PACK], F32, name="second_weights")
+        nc.vector.tensor_copy(out=second_weights[:], in_=weight_bank[:, 0 : 2 * PACK])
+        weights = [
+            [first_weights[side][:], second_weights[:, side * PACK : (side + 1) * PACK]] for side in range(2)
+        ]
+
+        def gather(name, table, offsets, start, count, sign):
+            picked = keep.tile([P, count], F32, name="%s_picked%d" % (name, start))
+            window = table[:].indirect(offsets[:, start // 16 : (start + count) // 16])
+            nc.scalar.activation(picked[:], window, ACT.Copy, scale=sign)
+            return picked
+
+        def turn_and_add(negated, own, bank):
+            terms = [(src, t) for src in (own, negated[:]) for t in range(PACK)]
+            for c, (src, t) in enumerate(terms):
+                nc.tensor.matmul(
+                    bank[:, t, :],
+                    lhsT=src[:, t:SPAN:PACK],
+                    rhs=ident[:],
+                    is_transpose=True,
+                    start=(c == 0),
+                    stop=(c == len(terms) - 1),
+                )
+
+        def subtract_and_turn(name, pieces, own, bank):
+            diff = keep.tile([P, PACK, P], F32, name="%s_diff" % name)
+            dealt = diff[:].rearrange("r t (g i) -> r g t i", i=RUN)
+            count = SPAN // len(pieces)
+            blocks = count // (PACK * RUN)
+            for c, picked in enumerate(pieces):
+                nc.vector.tensor_tensor(
+                    out=dealt[:, c * blocks : (c + 1) * blocks],
+                    in0=picked[:].rearrange("r (g t i) -> r g t i", t=PACK, i=RUN),
+                    in1=own[:, c * count : (c + 1) * count].rearrange("r (g t i) -> r g t i", t=PACK, i=RUN),
+                    op=ALU.subtract,
+                )
+            for t in range(PACK):
+                nc.tensor.transpose(bank[:, t, :], diff[:, t, :], ident[:])
+
+        def weigh(name, bank, factor, a):
+            rounded = keep.tile([P, P, PACK], BF16, name="%s_rounded%d" % (name, a), align_bytes=64)
+            nc.vector.tensor_tensor(
+                out=rounded[:],
+                in0=bank[:].rearrange("p t c -> p c t"),
+                in1=factor.unsqueeze(1).to_broadcast([P, P, PACK]),
+                op=ALU.mult,
+            )
+            return rounded
+
+        def quantize(rounded, codes, scales, fmt):
+            nc.vector.quantize_mx(out=codes.bitcast(fmt), scales=scales, in_=rounded[:].rearrange("p c t -> p (c t)"))
+
+        def operand(name, table, offsets, own, side, targets, fmt, last):
+            count = SPAN // 2 if last else SPAN
+            negated = gather(name, table, offsets, 0, SPAN, -1.0)
+            pieces = [gather(name, table, offsets, start, count, 1.0) for start in range(SPAN, J, count)]
+            banks = [
+                psum.tile([P, PACK, P], F32, name="bank", tag="last%d" % a if last else "ring", bufs=1 if last else 4)
+                for a in range(PASSES)
+            ]
+            turn_and_add(negated, own[0], banks[0])
+            subtract_and_turn(name, pieces, own[1], banks[1])
+            for a in range(PASSES):
+                rounded = weigh(name, banks[a], weights[side][a], a)
+                quantize(rounded, targets[a][0], targets[a][1], fmt)
+
+        g_codes = [keep.tile([P, N], U32, name="g_codes%d" % a, align_bytes=64) for a in range(PASSES)]
+        g_scales = [keep.tile([P, N], U8, name="g_scales%d" % a, align_bytes=64) for a in range(PASSES)]
+        for r, (table, own) in enumerate(((g_table0, g_own0), (g_table1, g_own1))):
+            targets = [(g_codes[a][:, rows(r)], g_scales[a][:, rows(r)]) for a in range(PASSES)]
+            operand("g%d" % r, table, g_list, own, 1, targets, E5M2X4, False)
+
+        u_operands = []
+        for r, (table, own) in enumerate(((x_table0, x_own0), (x_table1, x_own1))):
+            u_codes = [keep.tile([P, P], U32, name="u_codes%d_%d" % (r, a), align_bytes=64) for a in range(PASSES)]
+            u_scales = [keep.tile([P, P], U8, name="u_scales%d_%d" % (r, a), align_bytes=64) for a in range(PASSES)]
+            targets = [(u_codes[a][:], u_scales[a][:]) for a in range(PASSES)]
+            operand("x%d" % r, table, x_list, own, 0, targets, E4M3X4, r == K // P - 1)
+            u_operands.append(targets)
+
+        moments = []
+        for r in range(K // P):
+            moment = psum.tile([P, N], F32, name="moment%d" % r, tag="last%d" % r, bufs=1)
+            for a in range(PASSES):
+                nc.tensor.matmul_mx(
+                    out=moment[:],
+                    lhsT=u_operands[r][a][0].bitcast(E4M3X4),
+                    lhsT_scale=u_operands[r][a][1],
+                    rhs=g_codes[a][:].bitcast(E5M2X4),
+                    rhs_scale=g_scales[a][:],
+                    start=(a == 0),
+                    stop=(a == PASSES - 1),
+                )
+            moments.append(moment)
+
+        for r in reversed(range(K // P)):
+            moment = moments[r]
+            size = keep.tile([P, N], F32, name="size%d" % r)
+            nc.scalar.activation(size[:], moment[:], ACT.Abs)
+            divisor = keep.tile([P, 1], F32, name="divisor%d" % r)
+            nc.vector.tensor_scalar(
+                out=size[:], in0=size[:], scalar1=2.0, scalar2=None, op0=ALU.add, op1=ALU.max, accum_out=divisor[:]
+            )
+            inverse = keep.tile([P, 1], F32, name="inverse%d" % r)
+            nc.vector.reciprocal(inverse[:], divisor[:])
+            decay = keep.tile([P, N], F32, name="decay%d" % r)
+            nc.scalar.activation(decay[:], old_raw[:, r, :], ACT.Copy, scale=0.3)
+            result = keep.tile([P, N], F32, name="result%d" % r)
+            nc.vector.scalar_tensor_tensor(
+                out=result[:], in0=moment[:], scalar=inverse[:], in1=decay[:], op0=ALU.mult, op1=ALU.subtract
+            )
+            nc.sync.dma_start(out=out[rows(r), :], in_=result[:])

@@ -19,6 +19,8 @@ ACT = mybir.ActivationFunctionType
 P = 128
 PACK = 4
 RUN = 8
+QUAD = 32
+BLOCK = PACK * RUN
 SPAN = P * PACK
 PASSES = J // SPAN
 
@@ -50,24 +52,23 @@ def tile_list_moment_offset_errors_rowpeaks_kernel(tc, xf, ra, ow, gt, rb, pr, o
                 tiles.append(own)
             return [tiles[a * SPAN // width][:, a * SPAN % width : a * SPAN % width + SPAN] for a in range(PASSES)]
 
-        weight_rows = keep.tile([P, P], F32, name="weight_rows")
+        weight_rows = keep.tile([P, PACK, P], F32, name="weight_rows")
         nc.vector.memset(weight_rows[:], 0.0)
         ident = keep.tile([P, P], F32, name="ident")
         make_identity(nc, ident[:])
 
         g_table0 = load_table("g", gt, 0)
         nc.sync.dma_start(g_list[:], offs2)
-        weight_raw = keep.tile([P, P], F32, name="weight_raw")
-        first_weights = []
+        weight_raw = keep.tile([P, SPAN], F32, name="weight_raw")
         for side, vec in enumerate((ra, rb)):
-            first = keep.tile([P, PACK], F32, name="first_weights%d" % side)
-            nc.sync.dma_start(out=first[:], in_=vec[:, 0:SPAN].rearrange("o (p t) -> (o p) t", t=PACK))
-            first_weights.append(first)
             nc.sync.dma_start(
-                out=weight_raw[side * PACK : (side + 1) * PACK, :].rearrange("t (g i) -> t g i", i=RUN),
-                in_=vec[:, SPAN:J].rearrange("o (g t i) -> t (o g) i", t=PACK, i=RUN),
+                out=weight_raw[side : PASSES * QUAD : QUAD, :], in_=vec.rearrange("o (a j) -> (o a) j", a=PASSES)
             )
-        nc.vector.tensor_copy(out=weight_rows[0 : 2 * PACK, :], in_=weight_raw[0 : 2 * PACK, :])
+        nc.vector.tensor_copy(out=weight_rows[0:2], in_=weight_raw[0:2, :].rearrange("v (p t) -> v t p", t=PACK))
+        nc.vector.tensor_copy(
+            out=weight_rows[QUAD : QUAD + 2].rearrange("v t (g i) -> v t g i", i=RUN),
+            in_=weight_raw[QUAD : QUAD + 2, :].rearrange("v (g t i) -> v t g i", t=PACK, i=RUN),
+        )
         g_own0 = load_own("g", pr, 0, 1)
         g_table1 = load_table("g", gt, 1)
         g_own1 = load_own("g", pr, 1, 1)
@@ -79,13 +80,13 @@ def tile_list_moment_offset_errors_rowpeaks_kernel(tc, xf, ra, ow, gt, rb, pr, o
         old_raw = keep.tile([P, K // P, N], F32, name="old_raw")
         nc.sync.dma_start(out=old_raw[:], in_=old.rearrange("(r p) n -> p r n", p=P))
 
-        weight_bank = psum.tile([P, P], F32, name="weight_bank")
-        nc.tensor.transpose(weight_bank[:], weight_rows[:], ident[:])
-        second_weights = keep.tile([P, 2 * PACK], F32, name="second_weights")
-        nc.vector.tensor_copy(out=second_weights[:], in_=weight_bank[:, 0 : 2 * PACK])
-        weights = [
-            [first_weights[side][:], second_weights[:, side * PACK : (side + 1) * PACK]] for side in range(2)
-        ]
+        weight_bank = psum.tile([P, PACK, P], F32, name="weight_bank")
+        for t in range(PACK):
+            nc.tensor.transpose(weight_bank[:, t, :], weight_rows[:, t, :], ident[:])
+        weights = keep.tile([P, PASSES, 2, PACK], F32, name="weights")
+        nc.vector.tensor_copy(
+            out=weights[:], in_=weight_bank[:].rearrange("p t (a v) -> p a v t", v=QUAD)[:, 0:PASSES, 0:2, :]
+        )
 
         def gather(name, table, offsets, start, count, sign):
             picked = keep.tile([P, count], F32, name="%s_picked%d" % (name, start))
@@ -108,13 +109,11 @@ def tile_list_moment_offset_errors_rowpeaks_kernel(tc, xf, ra, ow, gt, rb, pr, o
         def subtract_and_turn(name, pieces, own, bank):
             diff = keep.tile([P, PACK, P], F32, name="%s_diff" % name)
             dealt = diff[:].rearrange("r t (g i) -> r g t i", i=RUN)
-            count = SPAN // len(pieces)
-            blocks = count // (PACK * RUN)
-            for c, picked in enumerate(pieces):
+            for start, count, picked in pieces:
                 nc.vector.tensor_tensor(
-                    out=dealt[:, c * blocks : (c + 1) * blocks],
+                    out=dealt[:, start // BLOCK : (start + count) // BLOCK],
                     in0=picked[:].rearrange("r (g t i) -> r g t i", t=PACK, i=RUN),
-                    in1=own[:, c * count : (c + 1) * count].rearrange("r (g t i) -> r g t i", t=PACK, i=RUN),
+                    in1=own[:, start : start + count].rearrange("r (g t i) -> r g t i", t=PACK, i=RUN),
                     op=ALU.subtract,
                 )
             for t in range(PACK):
@@ -134,9 +133,12 @@ def tile_list_moment_offset_errors_rowpeaks_kernel(tc, xf, ra, ow, gt, rb, pr, o
             nc.vector.quantize_mx(out=codes.bitcast(fmt), scales=scales, in_=rounded[:].rearrange("p c t -> p (c t)"))
 
         def operand(name, table, offsets, own, side, targets, fmt, last):
-            count = SPAN // 2 if last else SPAN
+            cuts = (0, SPAN // 2, 3 * SPAN // 4, SPAN) if last else (0, SPAN)
             negated = gather(name, table, offsets, 0, SPAN, -1.0)
-            pieces = [gather(name, table, offsets, start, count, 1.0) for start in range(SPAN, J, count)]
+            pieces = [
+                (start, stop - start, gather(name, table, offsets, SPAN + start, stop - start, 1.0))
+                for start, stop in zip(cuts, cuts[1:])
+            ]
             banks = [
                 psum.tile([P, PACK, P], F32, name="bank", tag="last%d" % a if last else "ring", bufs=1 if last else 4)
                 for a in range(PASSES)
@@ -144,7 +146,7 @@ def tile_list_moment_offset_errors_rowpeaks_kernel(tc, xf, ra, ow, gt, rb, pr, o
             turn_and_add(negated, own[0], banks[0])
             subtract_and_turn(name, pieces, own[1], banks[1])
             for a in range(PASSES):
-                rounded = weigh(name, banks[a], weights[side][a], a)
+                rounded = weigh(name, banks[a], weights[:, a, side, :], a)
                 quantize(rounded, targets[a][0], targets[a][1], fmt)
 
         g_codes = [keep.tile([P, N], U32, name="g_codes%d" % a, align_bytes=64) for a in range(PASSES)]

@@ -23,6 +23,12 @@ QUAD = 32
 BLOCK = PACK * RUN
 SPAN = P * PACK
 PASSES = J // SPAN
+PER_COLUMN = 16
+U_SIDE, G_SIDE = 0, 1
+SIDES = 2
+RING_BANKS = 4
+WHOLE_PASS = (0, SPAN)
+SHRINKING = (0, SPAN // 2, 3 * SPAN // 4, SPAN)
 
 
 def tile_list_moment_offset_errors_rowpeaks_kernel(tc, xf, ra, ow, gt, rb, pr, old, offs, offs2, out):
@@ -32,8 +38,8 @@ def tile_list_moment_offset_errors_rowpeaks_kernel(tc, xf, ra, ow, gt, rb, pr, o
         keep = ctx.enter_context(tc.tile_pool(name="keep", bufs=1))
         psum = ctx.enter_context(tc.psum_pool(name="psum", bufs=1))
 
-        x_list = lists.tile([P, J // 16], U16, name="x_list")
-        g_list = lists.tile([P, J // 16], U16, name="g_list")
+        x_list = lists.tile([P, J // PER_COLUMN], U16, name="x_list")
+        g_list = lists.tile([P, J // PER_COLUMN], U16, name="g_list")
 
         def rows(r):
             return slice(r * P, (r + 1) * P)
@@ -43,14 +49,10 @@ def tile_list_moment_offset_errors_rowpeaks_kernel(tc, xf, ra, ow, gt, rb, pr, o
             nc.sync.dma_start(out=table[:], in_=src[rows(r), :])
             return table
 
-        def load_own(name, src, r, pieces):
-            width = J // pieces
-            tiles = []
-            for c in range(pieces):
-                own = keep.tile([P, width], F32, name="%s_own%d_%d" % (name, r, c))
-                nc.sync.dma_start(out=own[:], in_=src[rows(r), c * width : (c + 1) * width])
-                tiles.append(own)
-            return [tiles[a * SPAN // width][:, a * SPAN % width : a * SPAN % width + SPAN] for a in range(PASSES)]
+        def load_own(name, src, r, passes):
+            own = keep.tile([P, len(passes) * SPAN], F32, name="%s_own%d_%d" % (name, r, passes.start))
+            nc.sync.dma_start(out=own[:], in_=src[rows(r), passes.start * SPAN : passes.stop * SPAN])
+            return [own[:, c * SPAN : (c + 1) * SPAN] for c in range(len(passes))]
 
         weight_rows = keep.tile([P, PACK, P], F32, name="weight_rows")
         nc.vector.memset(weight_rows[:], 0.0)
@@ -64,33 +66,36 @@ def tile_list_moment_offset_errors_rowpeaks_kernel(tc, xf, ra, ow, gt, rb, pr, o
             nc.sync.dma_start(
                 out=weight_raw[side : PASSES * QUAD : QUAD, :], in_=vec.rearrange("o (a j) -> (o a) j", a=PASSES)
             )
-        nc.vector.tensor_copy(out=weight_rows[0:2], in_=weight_raw[0:2, :].rearrange("v (p t) -> v t p", t=PACK))
         nc.vector.tensor_copy(
-            out=weight_rows[QUAD : QUAD + 2].rearrange("v t (g i) -> v t g i", i=RUN),
-            in_=weight_raw[QUAD : QUAD + 2, :].rearrange("v (g t i) -> v t g i", t=PACK, i=RUN),
+            out=weight_rows[0:SIDES], in_=weight_raw[0:SIDES, :].rearrange("v (p t) -> v t p", t=PACK)
         )
-        g_own0 = load_own("g", pr, 0, 1)
+        nc.vector.tensor_copy(
+            out=weight_rows[QUAD : QUAD + SIDES].rearrange("v t (g i) -> v t g i", i=RUN),
+            in_=weight_raw[QUAD : QUAD + SIDES, :].rearrange("v (g t i) -> v t g i", t=PACK, i=RUN),
+        )
+        g_own0 = load_own("g", pr, 0, range(PASSES))
         g_table1 = load_table("g", gt, 1)
-        g_own1 = load_own("g", pr, 1, 1)
+        g_own1 = load_own("g", pr, 1, range(PASSES))
         nc.sync.dma_start(x_list[:], offs)
         x_table0 = load_table("x", xf, 0)
-        x_own0 = load_own("x", ow, 0, 1)
+        x_own0 = load_own("x", ow, 0, range(PASSES))
+        x_own1_first = load_own("x", ow, 1, range(0, 1))
         x_table1 = load_table("x", xf, 1)
-        x_own1 = load_own("x", ow, 1, PASSES)
+        x_own1 = x_own1_first + load_own("x", ow, 1, range(1, PASSES))
         old_raw = keep.tile([P, K // P, N], F32, name="old_raw")
         nc.sync.dma_start(out=old_raw[:], in_=old.rearrange("(r p) n -> p r n", p=P))
 
         weight_bank = psum.tile([P, PACK, P], F32, name="weight_bank")
         for t in range(PACK):
             nc.tensor.transpose(weight_bank[:, t, :], weight_rows[:, t, :], ident[:])
-        weights = keep.tile([P, PASSES, 2, PACK], F32, name="weights")
+        weights = keep.tile([P, PASSES, SIDES, PACK], F32, name="weights")
         nc.vector.tensor_copy(
-            out=weights[:], in_=weight_bank[:].rearrange("p t (a v) -> p a v t", v=QUAD)[:, 0:PASSES, 0:2, :]
+            out=weights[:], in_=weight_bank[:].rearrange("p t (a v) -> p a v t", v=QUAD)[:, 0:PASSES, 0:SIDES, :]
         )
 
         def gather(name, table, offsets, start, count, sign):
             picked = keep.tile([P, count], F32, name="%s_picked%d" % (name, start))
-            window = table[:].indirect(offsets[:, start // 16 : (start + count) // 16])
+            window = table[:].indirect(offsets[:, start // PER_COLUMN : (start + count) // PER_COLUMN])
             nc.scalar.activation(picked[:], window, ACT.Copy, scale=sign)
             return picked
 
@@ -133,14 +138,16 @@ def tile_list_moment_offset_errors_rowpeaks_kernel(tc, xf, ra, ow, gt, rb, pr, o
             nc.vector.quantize_mx(out=codes.bitcast(fmt), scales=scales, in_=rounded[:].rearrange("p c t -> p (c t)"))
 
         def operand(name, table, offsets, own, side, targets, fmt, last):
-            cuts = (0, SPAN // 2, 3 * SPAN // 4, SPAN) if last else (0, SPAN)
+            cuts = SHRINKING if last else WHOLE_PASS
             negated = gather(name, table, offsets, 0, SPAN, -1.0)
             pieces = [
                 (start, stop - start, gather(name, table, offsets, SPAN + start, stop - start, 1.0))
                 for start, stop in zip(cuts, cuts[1:])
             ]
             banks = [
-                psum.tile([P, PACK, P], F32, name="bank", tag="last%d" % a if last else "ring", bufs=1 if last else 4)
+                psum.tile(
+                    [P, PACK, P], F32, name="bank", tag="last%d" % a if last else "ring", bufs=1 if last else RING_BANKS
+                )
                 for a in range(PASSES)
             ]
             turn_and_add(negated, own[0], banks[0])
@@ -153,14 +160,14 @@ def tile_list_moment_offset_errors_rowpeaks_kernel(tc, xf, ra, ow, gt, rb, pr, o
         g_scales = [keep.tile([P, N], U8, name="g_scales%d" % a, align_bytes=64) for a in range(PASSES)]
         for r, (table, own) in enumerate(((g_table0, g_own0), (g_table1, g_own1))):
             targets = [(g_codes[a][:, rows(r)], g_scales[a][:, rows(r)]) for a in range(PASSES)]
-            operand("g%d" % r, table, g_list, own, 1, targets, E5M2X4, False)
+            operand("g%d" % r, table, g_list, own, G_SIDE, targets, E5M2X4, False)
 
         u_operands = []
         for r, (table, own) in enumerate(((x_table0, x_own0), (x_table1, x_own1))):
             u_codes = [keep.tile([P, P], U32, name="u_codes%d_%d" % (r, a), align_bytes=64) for a in range(PASSES)]
             u_scales = [keep.tile([P, P], U8, name="u_scales%d_%d" % (r, a), align_bytes=64) for a in range(PASSES)]
             targets = [(u_codes[a][:], u_scales[a][:]) for a in range(PASSES)]
-            operand("x%d" % r, table, x_list, own, 0, targets, E4M3X4, r == K // P - 1)
+            operand("x%d" % r, table, x_list, own, U_SIDE, targets, E4M3X4, r == K // P - 1)
             u_operands.append(targets)
 
         moments = []

from contextlib import ExitStack

import concourse.mybir as mybir
from concourse.masks import make_identity

K, J, N, T = 256, 1024, 256, 2048
FLOPS = 2 * K * N * J

F32 = mybir.dt.float32
BF16 = mybir.dt.bfloat16
U32 = mybir.dt.uint32
U16 = mybir.dt.uint16
U8 = mybir.dt.uint8
E4M3X4 = mybir.dt.float8_e4m3fn_x4
E5M2X4 = mybir.dt.float8_e5m2_x4
ALU = mybir.AluOpType
ACT = mybir.ActivationFunctionType

P = 128
PACK = 4
RUN = 8
QUAD = 32
BLOCK = PACK * RUN
SPAN = P * PACK
PASSES = J // SPAN
PER_COLUMN = 16
U_SIDE, G_SIDE = 0, 1
SIDES = 2
RING_BANKS = 4
WHOLE_PASS = (0, SPAN)
SHRINKING = (0, SPAN // 2, 3 * SPAN // 4, SPAN)


def tile_list_moment_offset_errors_rowpeaks_kernel(tc, xf, ra, ow, gt, rb, pr, old, offs, offs2, out):
    nc = tc.nc
    with ExitStack() as ctx:
        lists = ctx.enter_context(tc.tile_pool(name="lists", bufs=1))
        keep = ctx.enter_context(tc.tile_pool(name="keep", bufs=1))
        psum = ctx.enter_context(tc.psum_pool(name="psum", bufs=1))

        x_list = lists.tile([P, J // PER_COLUMN], U16, name="x_list")
        g_list = lists.tile([P, J // PER_COLUMN], U16, name="g_list")

        def rows(r):
            return slice(r * P, (r + 1) * P)

        def load_table(name, src, r):
            table = keep.tile([P, T], F32, name="%s_table%d" % (name, r))
            nc.sync.dma_start(out=table[:], in_=src[rows(r), :])
            return table

        def load_own(name, src, r, passes):
            own = keep.tile([P, len(passes) * SPAN], F32, name="%s_own%d_%d" % (name, r, passes.start))
            nc.sync.dma_start(out=own[:], in_=src[rows(r), passes.start * SPAN : passes.stop * SPAN])
            return [own[:, c * SPAN : (c + 1) * SPAN] for c in range(len(passes))]

        weight_rows = keep.tile([P, PACK, P], F32, name="weight_rows")
        nc.vector.memset(weight_rows[:], 0.0)
        ident = keep.tile([P, P], F32, name="ident")
        make_identity(nc, ident[:])

        g_table0 = load_table("g", gt, 0)
        nc.sync.dma_start(g_list[:], offs2)
        weight_raw = keep.tile([P, SPAN], F32, name="weight_raw")
        for side, vec in enumerate((ra, rb)):
            nc.sync.dma_start(
                out=weight_raw[side : PASSES * QUAD : QUAD, :], in_=vec.rearrange("o (a j) -> (o a) j", a=PASSES)
            )
        nc.vector.tensor_copy(
            out=weight_rows[0:SIDES], in_=weight_raw[0:SIDES, :].rearrange("v (p t) -> v t p", t=PACK)
        )
        nc.vector.tensor_copy(
            out=weight_rows[QUAD : QUAD + SIDES].rearrange("v t (g i) -> v t g i", i=RUN),
            in_=weight_raw[QUAD : QUAD + SIDES, :].rearrange("v (g t i) -> v t g i", t=PACK, i=RUN),
        )
        g_own0 = load_own("g", pr, 0, range(PASSES))
        g_table1 = load_table("g", gt, 1)
        g_own1 = load_own("g", pr, 1, range(PASSES))
        nc.sync.dma_start(x_list[:], offs)
        x_table0 = load_table("x", xf, 0)
        x_own0 = load_own("x", ow, 0, range(PASSES))
        x_own1_first = load_own("x", ow, 1, range(0, 1))
        x_table1 = load_table("x", xf, 1)
        x_own1 = x_own1_first + load_own("x", ow, 1, range(1, PASSES))
        old_raw = keep.tile([P, K // P, N], F32, name="old_raw")
        nc.sync.dma_start(out=old_raw[:], in_=old.rearrange("(r p) n -> p r n", p=P))

        weight_bank = psum.tile([P, PACK, P], F32, name="weight_bank")
        for t in range(PACK):
            nc.tensor.transpose(weight_bank[:, t, :], weight_rows[:, t, :], ident[:])
        weights = keep.tile([P, PASSES, SIDES, PACK], F32, name="weights")
        nc.vector.tensor_copy(
            out=weights[:], in_=weight_bank[:].rearrange("p t (a v) -> p a v t", v=QUAD)[:, 0:PASSES, 0:SIDES, :]
        )

        def gather(name, table, offsets, start, count, sign):
            picked = keep.tile([P, count], F32, name="%s_picked%d" % (name, start))
            window = table[:].indirect(offsets[:, start // PER_COLUMN : (start + count) // PER_COLUMN])
            nc.scalar.activation(picked[:], window, ACT.Copy, scale=sign)
            return picked

        def turn_and_add(negated, own, bank):
            terms = [(src, t) for src in (own, negated[:]) for t in range(PACK)]
            for c, (src, t) in enumerate(terms):
                nc.tensor.matmul(
                    bank[:, t, :],
                    lhsT=src[:, t:SPAN:PACK],
                    rhs=ident[:],
                    is_transpose=True,
                    start=(c == 0),
                    stop=(c == len(terms) - 1),
                )

        def subtract_and_turn(name, pieces, own, bank):
            diff = keep.tile([P, PACK, P], F32, name="%s_diff" % name)
            dealt = diff[:].rearrange("r t (g i) -> r g t i", i=RUN)
            for start, count, picked in pieces:
                nc.vector.tensor_tensor(
                    out=dealt[:, start // BLOCK : (start + count) // BLOCK],
                    in0=picked[:].rearrange("r (g t i) -> r g t i", t=PACK, i=RUN),
                    in1=own[:, start : start + count].rearrange("r (g t i) -> r g t i", t=PACK, i=RUN),
                    op=ALU.subtract,
                )
            for t in range(PACK):
                nc.tensor.transpose(bank[:, t, :], diff[:, t, :], ident[:])

        def weigh(name, bank, factor, a):
            rounded = keep.tile([P, P, PACK], BF16, name="%s_rounded%d" % (name, a), align_bytes=64)
            nc.vector.tensor_tensor(
                out=rounded[:],
                in0=bank[:].rearrange("p t c -> p c t"),
                in1=factor.unsqueeze(1).to_broadcast([P, P, PACK]),
                op=ALU.mult,
            )
            return rounded

        def quantize(rounded, codes, scales, fmt):
            nc.vector.quantize_mx(out=codes.bitcast(fmt), scales=scales, in_=rounded[:].rearrange("p c t -> p (c t)"))

        def operand(name, table, offsets, own, side, targets, fmt, last):
            cuts = SHRINKING if last else WHOLE_PASS
            negated = gather(name, table, offsets, 0, SPAN, -1.0)
            pieces = [
                (start, stop - start, gather(name, table, offsets, SPAN + start, stop - start, 1.0))
                for start, stop in zip(cuts, cuts[1:])
            ]
            banks = [
                psum.tile(
                    [P, PACK, P], F32, name="bank", tag="last%d" % a if last else "ring", bufs=1 if last else RING_BANKS
                )
                for a in range(PASSES)
            ]
            turn_and_add(negated, own[0], banks[0])
            subtract_and_turn(name, pieces, own[1], banks[1])
            for a in range(PASSES):
                rounded = weigh(name, banks[a], weights[:, a, side, :], a)
                quantize(rounded, targets[a][0], targets[a][1], fmt)

        g_codes = [keep.tile([P, N], U32, name="g_codes%d" % a, align_bytes=64) for a in range(PASSES)]
        g_scales = [keep.tile([P, N], U8, name="g_scales%d" % a, align_bytes=64) for a in range(PASSES)]
        for r, (table, own) in enumerate(((g_table0, g_own0), (g_table1, g_own1))):
            targets = [(g_codes[a][:, rows(r)], g_scales[a][:, rows(r)]) for a in range(PASSES)]
            operand("g%d" % r, table, g_list, own, G_SIDE, targets, E5M2X4, False)

        u_operands = []
        for r, (table, own) in enumerate(((x_table0, x_own0), (x_table1, x_own1))):
            u_codes = [keep.tile([P, P], U32, name="u_codes%d_%d" % (r, a), align_bytes=64) for a in range(PASSES)]
            u_scales = [keep.tile([P, P], U8, name="u_scales%d_%d" % (r, a), align_bytes=64) for a in range(PASSES)]
            targets = [(u_codes[a][:], u_scales[a][:]) for a in range(PASSES)]
            operand("x%d" % r, table, x_list, own, U_SIDE, targets, E4M3X4, r == K // P - 1)
            u_operands.append(targets)

        moments = []
        for r in range(K // P):
            moment = psum.tile([P, N], F32, name="moment%d" % r, tag="last%d" % r, bufs=1)
            for a in range(PASSES):
                nc.tensor.matmul_mx(
                    out=moment[:],
                    lhsT=u_operands[r][a][0].bitcast(E4M3X4),
                    lhsT_scale=u_operands[r][a][1],
                    rhs=g_codes[a][:].bitcast(E5M2X4),
                    rhs_scale=g_scales[a][:],
                    start=(a == 0),
                    stop=(a == PASSES - 1),
                )
            moments.append(moment)

        for r in reversed(range(K // P)):
            moment = moments[r]
            size = keep.tile([P, N], F32, name="size%d" % r)
            nc.scalar.activation(size[:], moment[:], ACT.Abs)
            divisor = keep.tile([P, 1], F32, name="divisor%d" % r)
            nc.vector.tensor_scalar(
                out=size[:], in0=size[:], scalar1=2.0, scalar2=None, op0=ALU.add, op1=ALU.max, accum_out=divisor[:]
            )
            inverse = keep.tile([P, 1], F32, name="inverse%d" % r)
            nc.vector.reciprocal(inverse[:], divisor[:])
            decay = keep.tile([P, N], F32, name="decay%d" % r)
            nc.scalar.activation(decay[:], old_raw[:, r, :], ACT.Copy, scale=0.3)
            result = keep.tile([P, N], F32, name="result%d" % r)
            nc.vector.scalar_tensor_tensor(
                out=result[:], in0=moment[:], scalar=inverse[:], in1=decay[:], op0=ALU.mult, op1=ALU.subtract
            )
            nc.sync.dma_start(out=out[rows(r), :], in_=result[:])
